import numpy as np, ml_dtypes
CORES = [34,162,290,418,42,426]
N = 6
GR, GC = 2, 3
L, KA, KB, F = 6, 2, 3, 32
def setup_inputs(rng):
    return {"a": rng.standard_normal((N, 128, KA * 128), dtype=np.float32).astype(ml_dtypes.bfloat16), "b": rng.standard_normal((N, 128, KB * F), dtype=np.float32).astype(ml_dtypes.bfloat16)}
def setup_inputs_big(rng):
    d = setup_inputs(rng)
    for k in ("a", "b"): d[k] = (d[k].astype(np.float32) * 1024.0).astype(d[k].dtype)
    return d
def setup_inputs_small(rng):
    d = setup_inputs(rng)
    for k in ("a", "b"): d[k] = (d[k].astype(np.float32) * (1 / 1024.0)).astype(d[k].dtype)
    return d
def setup_inputs_apart(rng):
    d = setup_inputs(rng)
    f = (10.0 ** rng.permutation(np.linspace(-1.5, 1.5, N))).astype(np.float32).reshape(N, 1, 1)
    for k in ("a", "b"): d[k] = (d[k].astype(np.float32) * f).astype(d[k].dtype)
    return d
def reference(a, b):
    A, B = a.astype(np.float64), b.astype(np.float64)
    y = np.zeros((N, 128, F))
    for i in range(GR):
        for j in range(GC):
            for k in range(L):
                At = A[i * GC + k // KA][:, 128 * (k % KA):128 * (k % KA) + 128]
                Bt = B[(k // KB) * GC + j][:, F * (k % KB):F * (k % KB) + F]
                y[i * GC + j] += At.T @ Bt
    return {"y": y.astype(ml_dtypes.bfloat16 if a.dtype != np.float64 else np.float64)}

@@ -1,0 +1,210 @@
+from concourse.bass import DstId, RemoteDMATransfer
+from concourse.mybir import AluOpType
+
+N, GR, GC = 6, 2, 3
+L, KA, KB, F = 6, 2, 3, 32
+P = 128
+WA, WB = KA * P, KB * F
+SLOT = WA + WB
+
+SCRATCH = {
+    "ab": ("sbuf", [P, N * SLOT], "bfloat16"),
+    "pout": ("sbuf", [P, F], "bfloat16"),
+    "pin": ("sbuf", [P, F], "bfloat16"),
+    "yo": ("sbuf", [P, F], "bfloat16"),
+    "accy": ("psum", [P, 512], "float32"),
+    "accp": ("psum", [P, 512], "float32"),
+}
+SEMAPHORES = (["lda", "ldb", "sent", "rp", "mmp", "cpp", "mmy", "yv", "st"]
+              + ["ra%d" % s for s in range(N)] + ["rb%d" % s for s in range(N)])
+
+
+def a_home(i, k):
+    return i * GC + k // KA
+
+
+def b_home(k, j):
+    return (k // KB) * GC + j
+
+
+def engine_list(mask):
+    return [e for e in range(mask.bit_length()) if (mask >> e) & 1]
+
+
+def to_mask(engines):
+    m = 0
+    for e in engines:
+        m |= 1 << e
+    return m
+
+
+def make_plan(cores, topo):
+    def ok(s, d):
+        return s == d or topo.may_write(cores[s], cores[d])
+
+    need = {}
+    own = dict((r, []) for r in range(N))
+    parts = {}
+
+    def operands(x, i, j, k):
+        return (("a", a_home(i, k), x, k % KA), ("b", b_home(k, j), x, k % KB))
+
+    def further_bytes(x, i, j, k):
+        n = 0
+        for kind, s, d, t in operands(x, i, j, k):
+            if s != d and t not in need.get((kind, s, d), [()])[0]:
+                n += 2 * P * (P if kind == "a" else F)
+        return n
+
+    def book(x, i, j, k, urgent):
+        for kind, s, d, t in operands(x, i, j, k):
+            if s != d:
+                e = need.setdefault((kind, s, d), [set(), False])
+                e[0].add(t)
+                e[1] = e[1] or urgent
+
+    on_the_way = []
+    for i in range(GR):
+        for j in range(GC):
+            for k in range(L):
+                d = i * GC + j
+                if ok(a_home(i, k), d) and ok(b_home(k, j), d):
+                    own[d].append(k)
+                    book(d, i, j, k, False)
+                else:
+                    on_the_way.append((i, j, k))
+    for i, j, k in on_the_way:
+        d = i * GC + j
+        sites = [x for x in range(N) if x != d and ok(x, d) and ok(a_home(i, k), x) and ok(b_home(k, j), x)]
+        x = min(sites, key=lambda x: (further_bytes(x, i, j, k), x))
+        parts.setdefault((x, d), []).append(k)
+        book(x, i, j, k, True)
+    assert all(sum(1 for q in parts if q[0] == r) <= 1 and sum(1 for q in parts if q[1] == r) <= 1 for r in range(N))
+
+    calls = dict((s, []) for s in range(N))
+    count, eta = {}, {}
+    for s in range(N):
+        items = []
+        for (kind, src, d), (tiles, urgent) in need.items():
+            if src == s:
+                base, w = (0, P) if kind == "a" else (WA, F)
+                items.append((not urgent, w * (max(tiles) + 1 - min(tiles)), kind, d, base + w * min(tiles)))
+        items.sort()
+        groups = []
+        for late, width, kind, d, lo in items:
+            if late and groups and groups[-1][0][0] and groups[-1][0][1:3] == (width, kind) and groups[-1][0][4] == lo:
+                groups[-1].append((late, width, kind, d, lo))
+            else:
+                groups.append([(late, width, kind, d, lo)])
+        clock = 0
+        for grp in groups:
+            free = None
+            for it in grp:
+                e = set(engine_list(topo.mask(cores[s], cores[it[3]])))
+                free = e if free is None else free & e
+            free = sorted(free)
+            each = 1
+            while each * 2 * len(grp) <= len(free):
+                each *= 2
+            call = []
+            for n, (late, width, kind, d, lo) in enumerate(grp):
+                eng = free[n::len(free) // each][:each]
+                call.append((kind, lo, lo + width, d, eng))
+                count[(kind, s, d)] = each
+                clock += 512 + 2 * width
+            for it in call:
+                eta[(it[0], s, it[3])] = clock
+            calls[s].append(call)
+    return own, parts, calls, count, eta
+
+
+def rank_program(g, core, T, topo):
+    r = T.rank_of(core)
+    if r is None:
+        return
+    cores, sem, ab = T.cores, T.sem, T.ab
+    own, parts, calls, count, eta = make_plan(cores, topo)
+    mine = r * SLOT
+    give = [(d, ks) for (x, d), ks in parts.items() if x == r]
+    take = [x for (x, d) in parts if d == r]
+
+    g.sync.dma_start(ab[:, mine:mine + WA], T.a[:, :]).then_inc(sem.lda, 16)
+    g.scalar.dma_start(ab[:, mine + WA:mine + SLOT], T.b[:, :]).then_inc(sem.ldb, 16)
+
+    sent, loaded = 0, set()
+    for call in calls[r]:
+        kind = call[0][0]
+        if kind not in loaded:
+            loaded.add(kind)
+            g.wait_ge(sem["ld" + kind], 16)
+        if len(call) == 1:
+            kind, lo, hi, d, eng = call[0]
+            rid, pid = topo.addr(cores[d], core)
+            g.remote_dma(ab[:, mine + lo:mine + hi], ab[:, mine + lo:mine + hi], sem["r%s%d" % (kind, r)], sem.sent,
+                         pid, rid, to_mask(eng))
+            sent += len(eng)
+        else:
+            trs = []
+            for kind, lo, hi, d, eng in call:
+                rid, pid = topo.addr(cores[d], core)
+                trs.append(RemoteDMATransfer(dst_ids=[DstId(rid=rid, pnc=pid)], dma_engine_mask=to_mask(eng),
+                                             remote_sem=sem["r%s%d" % (kind, r)],
+                                             src=ab[:, mine + lo:mine + hi], dst=ab[:, mine + lo:mine + hi]))
+                sent += len(eng)
+            g.remote_dma_fused(trs, local_sem=sem.sent)
+    p_engines = {}
+    for (x, d) in parts:
+        p_engines[d] = engine_list(topo.mask(cores[x], cores[d]))
+    for d, ks in give:
+        rid, pid = topo.addr(cores[d], core)
+        g.wait_ge(sem.cpp, 1)
+        g.remote_dma(T.pin[:, :], T.pout[:, :], sem.rp, sem.sent, pid, rid, to_mask(p_engines[d]))
+        sent += len(p_engines[d])
+    g.wait_ge(sem.sent, sent)
+
+    jobs = []
+    for k in own[r]:
+        jobs.append(("y", r // GC, r % GC, k))
+    for d, ks in give:
+        for k in ks:
+            jobs.append(("p", d // GC, d % GC, k))
+
+    def when(job):
+        grp, i, j, k = job
+        t = max(eta.get(("a", a_home(i, k), r), 0), eta.get(("b", b_home(k, j), r), 0))
+        return (0, 0, k) if t == 0 else (1, 0, k) if grp == "p" else (2, t, k)
+
+    jobs.sort(key=when)
+    waited = set()
+    left = {"y": len(own[r]), "p": len(jobs) - len(own[r])}
+    total = dict(left)
+    for grp, i, j, k in jobs:
+        for kind, s in (("a", a_home(i, k)), ("b", b_home(k, j))):
+            if (kind, s) not in waited:
+                waited.add((kind, s))
+                if s == r:
+                    g.tensor.wait_ge(sem["ld" + kind], 16)
+                else:
+                    g.tensor.wait_ge(sem["r%s%d" % (kind, s)], count[(kind, s, r)])
+        ca = a_home(i, k) * SLOT + P * (k % KA)
+        cb = b_home(k, j) * SLOT + WA + F * (k % KB)
+        acc = T.accy if grp == "y" else T.accp
+        first = left[grp] == total[grp]
+        left[grp] -= 1
+        mm = g.tensor.matmul(acc[:, 0:F], ab[:, ca:ca + P], ab[:, cb:cb + F], first, left[grp] == 0)
+        if left[grp] == 0:
+            mm.then_inc(sem.mmy if grp == "y" else sem.mmp, 1)
+
+    if give:
+        g.vector.wait_ge(sem.mmp, 1)
+        g.vector.tensor_copy(T.pout[:, :], T.accp[:, 0:F]).then_inc(sem.cpp, 1)
+    g.vector.wait_ge(sem.mmy, 1)
+    if take:
+        g.vector.wait_ge(sem.rp, len(p_engines[r]))
+        g.vector.tensor_tensor(T.yo[:, :], T.accy[:, 0:F], T.pin[:, :], AluOpType.add).then_inc(sem.yv, 1)
+    else:
+        g.vector.tensor_copy(T.yo[:, :], T.accy[:, 0:F]).then_inc(sem.yv, 1)
+
+    g.sync.wait_ge(sem.yv, 1)
+    g.sync.dma_start(T.y[:, :], T.yo[:, :]).then_inc(sem.st, 16)
+    g.sync.wait_ge(sem.st, 16)

@@ -6,17 +6,21 @@ L, KA, KB, F = 6, 2, 3, 32
 P = 128
 WA, WB = KA * P, KB * F
 SLOT = WA + WB
+NP = 2
 
 SCRATCH = {
     "ab": ("sbuf", [P, N * SLOT], "bfloat16"),
-    "pout": ("sbuf", [P, F], "bfloat16"),
-    "pin": ("sbuf", [P, F], "bfloat16"),
+    "pout": ("sbuf", [P, NP * F], "bfloat16"),
+    "pin": ("sbuf", [P, N * F], "bfloat16"),
+    "tmp": ("sbuf", [P, F], "float32"),
     "yo": ("sbuf", [P, F], "bfloat16"),
     "accy": ("psum", [P, 512], "float32"),
-    "accp": ("psum", [P, 512], "float32"),
+    "accp0": ("psum", [P, 512], "float32"),
+    "accp1": ("psum", [P, 512], "float32"),
 }
-SEMAPHORES = (["lda", "ldb", "sent", "rp", "mmp", "cpp", "mmy", "yv", "st"]
-              + ["ra%d" % s for s in range(N)] + ["rb%d" % s for s in range(N)])
+SEMAPHORES = (["lda", "ldb", "sent", "mmy", "yt", "yv", "st"]
+              + ["mmp%d" % n for n in range(NP)] + ["cpp%d" % n for n in range(NP)]
+              + ["r%s%d" % (q, s) for q in "abmp" for s in range(N)])
 
 
 def a_home(i, k):
@@ -54,68 +58,66 @@ def make_plan(cores, topo):
         for kind, s, d, t in operands(x, i, j, k):
             if s != d and t not in need.get((kind, s, d), [()])[0]:
                 n += 2 * P * (P if kind == "a" else F)
+        if x != i * GC + j and (x, i * GC + j) not in parts:
+            n += 2 * P * F
         return n
 
-    def book(x, i, j, k, urgent):
-        for kind, s, d, t in operands(x, i, j, k):
-            if s != d:
-                e = need.setdefault((kind, s, d), [set(), False])
-                e[0].add(t)
-                e[1] = e[1] or urgent
+    def sites(i, j, k):
+        return [x for x in range(N) if ok(x, i * GC + j) and ok(a_home(i, k), x) and ok(b_home(k, j), x)]
 
-    on_the_way = []
-    for i in range(GR):
-        for j in range(GC):
-            for k in range(L):
-                d = i * GC + j
-                if ok(a_home(i, k), d) and ok(b_home(k, j), d):
-                    own[d].append(k)
-                    book(d, i, j, k, False)
-                else:
-                    on_the_way.append((i, j, k))
-    for i, j, k in on_the_way:
+    terms = [(i, j, k) for i in range(GR) for j in range(GC) for k in range(L)]
+    terms.sort(key=lambda t: t[0] * GC + t[1] in sites(*t))
+    for i, j, k in terms:
         d = i * GC + j
-        sites = [x for x in range(N) if x != d and ok(x, d) and ok(a_home(i, k), x) and ok(b_home(k, j), x)]
-        x = min(sites, key=lambda x: (further_bytes(x, i, j, k), x))
-        parts.setdefault((x, d), []).append(k)
-        book(x, i, j, k, True)
-    assert all(sum(1 for q in parts if q[0] == r) <= 1 and sum(1 for q in parts if q[1] == r) <= 1 for r in range(N))
+        x = min(sites(i, j, k), key=lambda x: (further_bytes(x, i, j, k), x != d, x))
+        if x == d:
+            own[d].append(k)
+        else:
+            parts.setdefault((x, d), []).append(k)
+        for kind, s, q, t in operands(x, i, j, k):
+            if s != q:
+                e = need.setdefault((kind, s, q), [set(), False])
+                e[0].add(t)
+                e[1] = e[1] or x != d
+    assert all(sum(1 for q in parts if q[0] == r) <= NP and sum(1 for q in parts if q[1] == r) <= NP for r in range(N))
 
     calls = dict((s, []) for s in range(N))
-    count, eta = {}, {}
+    land, eta = {}, {}
     for s in range(N):
-        items = []
-        for (kind, src, d), (tiles, urgent) in need.items():
-            if src == s:
-                base, w = (0, P) if kind == "a" else (WA, F)
-                items.append((not urgent, w * (max(tiles) + 1 - min(tiles)), kind, d, base + w * min(tiles)))
-        items.sort()
-        groups = []
-        for late, width, kind, d, lo in items:
-            if late and groups and groups[-1][0][0] and groups[-1][0][1:3] == (width, kind) and groups[-1][0][4] == lo:
-                groups[-1].append((late, width, kind, d, lo))
-            else:
-                groups.append([(late, width, kind, d, lo)])
+        groups = {}
+        for d in range(N):
+            ea, eb = need.get(("a", s, d)), need.get(("b", s, d))
+            rng = {}
+            if ea:
+                rng["a"] = (P * min(ea[0]), P * (max(ea[0]) + 1), ea[1])
+            if eb:
+                rng["b"] = (WA + F * min(eb[0]), WA + F * (max(eb[0]) + 1), eb[1])
+            if ea and eb and rng["a"][1] == rng["b"][0] and ea[1] == eb[1]:
+                rng = {"m": (rng["a"][0], rng["b"][1], ea[1])}
+            for kind, (lo, hi, urgent) in rng.items():
+                e = groups.setdefault((kind, lo, hi - lo), [False, []])
+                e[0] = e[0] or urgent
+                e[1].append(d)
         clock = 0
-        for grp in groups:
+        for (kind, lo, width), (urgent, dsts) in sorted(groups.items(), key=lambda q: (not q[1][0], q[0][2], q[0])):
             free = None
-            for it in grp:
-                e = set(engine_list(topo.mask(cores[s], cores[it[3]])))
+            for d in dsts:
+                e = set(engine_list(topo.mask(cores[s], cores[d])))
                 free = e if free is None else free & e
             free = sorted(free)
             each = 1
-            while each * 2 * len(grp) <= len(free):
+            while each * 2 * len(dsts) <= len(free):
                 each *= 2
             call = []
-            for n, (late, width, kind, d, lo) in enumerate(grp):
-                eng = free[n::len(free) // each][:each]
-                call.append((kind, lo, lo + width, d, eng))
-                count[(kind, s, d)] = each
+            for n, d in enumerate(dsts):
+                call.append((kind, lo, lo + width, d, free[n::len(free) // each][:each]))
                 clock += 512 + 2 * width
             for it in call:
-                eta[(it[0], s, it[3])] = clock
+                for q in ("ab" if kind == "m" else kind):
+                    land[(q, s, it[3])] = ("r%s%d" % (kind, s), each)
+                    eta[(q, s, it[3])] = clock
             calls[s].append(call)
-    return own, parts, calls, count, eta
+    return own, parts, calls, land, eta
 
 
 def rank_program(g, core, T, topo):
@@ -123,20 +125,29 @@ def rank_program(g, core, T, topo):
     if r is None:
         return
     cores, sem, ab = T.cores, T.sem, T.ab
-    own, parts, calls, count, eta = make_plan(cores, topo)
+    own, parts, calls, land, eta = make_plan(cores, topo)
     mine = r * SLOT
-    give = [(d, ks) for (x, d), ks in parts.items() if x == r]
-    take = [x for (x, d) in parts if d == r]
+
+    def when(x, d, k):
+        return max(eta.get(("a", a_home(d // GC, k), x), 0), eta.get(("b", b_home(k, d % GC), x), 0))
+
+    def ready(x, d):
+        return max(when(x, d, k) for k in parts[(x, d)])
+
+    give = sorted((ready(x, d), d) for (x, d) in parts if x == r)
+    give = [d for t, d in give]
+    take = sorted((ready(x, d), x) for (x, d) in parts if d == r)
+    take = [x for t, x in take]
 
     g.sync.dma_start(ab[:, mine:mine + WA], T.a[:, :]).then_inc(sem.lda, 16)
     g.scalar.dma_start(ab[:, mine + WA:mine + SLOT], T.b[:, :]).then_inc(sem.ldb, 16)
 
     sent, loaded = 0, set()
     for call in calls[r]:
-        kind = call[0][0]
-        if kind not in loaded:
-            loaded.add(kind)
-            g.wait_ge(sem["ld" + kind], 16)
+        for q in ("ab" if call[0][0] == "m" else call[0][0]):
+            if q not in loaded:
+                loaded.add(q)
+                g.wait_ge(sem["ld" + q], 16)
         if len(call) == 1:
             kind, lo, hi, d, eng = call[0]
             rid, pid = topo.addr(cores[d], core)
@@ -152,58 +163,56 @@ def rank_program(g, core, T, topo):
                                              src=ab[:, mine + lo:mine + hi], dst=ab[:, mine + lo:mine + hi]))
                 sent += len(eng)
             g.remote_dma_fused(trs, local_sem=sem.sent)
-    p_engines = {}
-    for (x, d) in parts:
-        p_engines[d] = engine_list(topo.mask(cores[x], cores[d]))
-    for d, ks in give:
+    for n, d in enumerate(give):
+        eng = engine_list(topo.mask(core, cores[d]))
         rid, pid = topo.addr(cores[d], core)
-        g.wait_ge(sem.cpp, 1)
-        g.remote_dma(T.pin[:, :], T.pout[:, :], sem.rp, sem.sent, pid, rid, to_mask(p_engines[d]))
-        sent += len(p_engines[d])
+        g.wait_ge(sem["cpp%d" % n], 1)
+        g.remote_dma(T.pin[:, r * F:(r + 1) * F], T.pout[:, n * F:(n + 1) * F], sem["rp%d" % r], sem.sent,
+                     pid, rid, to_mask(eng))
+        sent += len(eng)
     g.wait_ge(sem.sent, sent)
 
     jobs = []
-    for k in own[r]:
-        jobs.append(("y", r // GC, r % GC, k))
-    for d, ks in give:
-        for k in ks:
-            jobs.append(("p", d // GC, d % GC, k))
-
-    def when(job):
-        grp, i, j, k = job
-        t = max(eta.get(("a", a_home(i, k), r), 0), eta.get(("b", b_home(k, j), r), 0))
-        return (0, 0, k) if t == 0 else (1, 0, k) if grp == "p" else (2, t, k)
-
-    jobs.sort(key=when)
-    waited = set()
-    left = {"y": len(own[r]), "p": len(jobs) - len(own[r])}
+    for n, d in enumerate(give):
+        jobs += [(0, when(r, d, k), n, d, k) for k in parts[(r, d)]]
+    jobs += [(1, when(r, r, k), NP, r, k) for k in own[r]]
+    jobs.sort()
+    left = {}
+    for job in jobs:
+        left[job[2]] = left.get(job[2], 0) + 1
     total = dict(left)
-    for grp, i, j, k in jobs:
+    waited = set()
+    for late, t, n, d, k in jobs:
+        i, j = d // GC, d % GC
         for kind, s in (("a", a_home(i, k)), ("b", b_home(k, j))):
-            if (kind, s) not in waited:
-                waited.add((kind, s))
-                if s == r:
-                    g.tensor.wait_ge(sem["ld" + kind], 16)
-                else:
-                    g.tensor.wait_ge(sem["r%s%d" % (kind, s)], count[(kind, s, r)])
+            name, cnt = ("ld" + kind, 16) if s == r else land[(kind, s, r)]
+            if name not in waited:
+                waited.add(name)
+                g.tensor.wait_ge(sem[name], cnt)
         ca = a_home(i, k) * SLOT + P * (k % KA)
         cb = b_home(k, j) * SLOT + WA + F * (k % KB)
-        acc = T.accy if grp == "y" else T.accp
-        first = left[grp] == total[grp]
-        left[grp] -= 1
-        mm = g.tensor.matmul(acc[:, 0:F], ab[:, ca:ca + P], ab[:, cb:cb + F], first, left[grp] == 0)
-        if left[grp] == 0:
-            mm.then_inc(sem.mmy if grp == "y" else sem.mmp, 1)
+        acc = T.accy if n == NP else T["accp%d" % n]
+        first = left[n] == total[n]
+        left[n] -= 1
+        mm = g.tensor.matmul(acc[:, 0:F], ab[:, ca:ca + P], ab[:, cb:cb + F], first, left[n] == 0)
+        if left[n] == 0:
+            mm.then_inc(sem.mmy if n == NP else sem["mmp%d" % n], 1)
 
-    if give:
-        g.vector.wait_ge(sem.mmp, 1)
-        g.vector.tensor_copy(T.pout[:, :], T.accp[:, 0:F]).then_inc(sem.cpp, 1)
+    for n, d in enumerate(give):
+        g.vector.wait_ge(sem["mmp%d" % n], 1)
+        g.vector.tensor_copy(T.pout[:, n * F:(n + 1) * F], T["accp%d" % n][:, 0:F]).then_inc(sem["cpp%d" % n], 1)
     g.vector.wait_ge(sem.mmy, 1)
-    if take:
-        g.vector.wait_ge(sem.rp, len(p_engines[r]))
-        g.vector.tensor_tensor(T.yo[:, :], T.accy[:, 0:F], T.pin[:, :], AluOpType.add).then_inc(sem.yv, 1)
-    else:
-        g.vector.tensor_copy(T.yo[:, :], T.accy[:, 0:F]).then_inc(sem.yv, 1)
+    src = T.accy[:, 0:F]
+    for n, x in enumerate(take):
+        g.vector.wait_ge(sem["rp%d" % x], len(engine_list(topo.mask(cores[x], core))))
+        if n + 1 < len(take):
+            g.vector.tensor_tensor(T.tmp[:, :], src, T.pin[:, x * F:(x + 1) * F], AluOpType.add).then_inc(sem.yt, 1)
+            g.vector.wait_ge(sem.yt, n + 1)
+            src = T.tmp[:, :]
+        else:
+            g.vector.tensor_tensor(T.yo[:, :], src, T.pin[:, x * F:(x + 1) * F], AluOpType.add).then_inc(sem.yv, 1)
+    if not take:
+        g.vector.tensor_copy(T.yo[:, :], src).then_inc(sem.yv, 1)
 
     g.sync.wait_ge(sem.yv, 1)
     g.sync.dma_start(T.y[:, :], T.yo[:, :]).then_inc(sem.st, 16)

from concourse.bass import DstId, RemoteDMATransfer
from concourse.mybir import AluOpType

N, GR, GC = 6, 2, 3
L, KA, KB, F = 6, 2, 3, 32
P = 128
WA, WB = KA * P, KB * F
SLOT = WA + WB
NP = 2

SCRATCH = {
    "ab": ("sbuf", [P, N * SLOT], "bfloat16"),
    "pout": ("sbuf", [P, NP * F], "bfloat16"),
    "pin": ("sbuf", [P, N * F], "bfloat16"),
    "tmp": ("sbuf", [P, F], "float32"),
    "yo": ("sbuf", [P, F], "bfloat16"),
    "accy": ("psum", [P, 512], "float32"),
    "accp0": ("psum", [P, 512], "float32"),
    "accp1": ("psum", [P, 512], "float32"),
}
SEMAPHORES = (["lda", "ldb", "sent", "mmy", "yt", "yv", "st"]
              + ["mmp%d" % n for n in range(NP)] + ["cpp%d" % n for n in range(NP)]
              + ["r%s%d" % (q, s) for q in "abmp" for s in range(N)])


def a_home(i, k):
    return i * GC + k // KA


def b_home(k, j):
    return (k // KB) * GC + j


def engine_list(mask):
    return [e for e in range(mask.bit_length()) if (mask >> e) & 1]


def to_mask(engines):
    m = 0
    for e in engines:
        m |= 1 << e
    return m


def make_plan(cores, topo):
    def ok(s, d):
        return s == d or topo.may_write(cores[s], cores[d])

    need = {}
    own = dict((r, []) for r in range(N))
    parts = {}

    def operands(x, i, j, k):
        return (("a", a_home(i, k), x, k % KA), ("b", b_home(k, j), x, k % KB))

    def further_bytes(x, i, j, k):
        n = 0
        for kind, s, d, t in operands(x, i, j, k):
            if s != d and t not in need.get((kind, s, d), [()])[0]:
                n += 2 * P * (P if kind == "a" else F)
        if x != i * GC + j and (x, i * GC + j) not in parts:
            n += 2 * P * F
        return n

    def sites(i, j, k):
        return [x for x in range(N) if ok(x, i * GC + j) and ok(a_home(i, k), x) and ok(b_home(k, j), x)]

    terms = [(i, j, k) for i in range(GR) for j in range(GC) for k in range(L)]
    terms.sort(key=lambda t: t[0] * GC + t[1] in sites(*t))
    for i, j, k in terms:
        d = i * GC + j
        x = min(sites(i, j, k), key=lambda x: (further_bytes(x, i, j, k), x != d, x))
        if x == d:
            own[d].append(k)
        else:
            parts.setdefault((x, d), []).append(k)
        for kind, s, q, t in operands(x, i, j, k):
            if s != q:
                e = need.setdefault((kind, s, q), [set(), False])
                e[0].add(t)
                e[1] = e[1] or x != d
    assert all(sum(1 for q in parts if q[0] == r) <= NP and sum(1 for q in parts if q[1] == r) <= NP for r in range(N))

    calls = dict((s, []) for s in range(N))
    land, eta = {}, {}
    for s in range(N):
        groups = {}
        for d in range(N):
            ea, eb = need.get(("a", s, d)), need.get(("b", s, d))
            rng = {}
            if ea:
                rng["a"] = (P * min(ea[0]), P * (max(ea[0]) + 1), ea[1])
            if eb:
                rng["b"] = (WA + F * min(eb[0]), WA + F * (max(eb[0]) + 1), eb[1])
            if ea and eb and rng["a"][1] == rng["b"][0] and ea[1] == eb[1]:
                rng = {"m": (rng["a"][0], rng["b"][1], ea[1])}
            for kind, (lo, hi, urgent) in rng.items():
                e = groups.setdefault((kind, lo, hi - lo), [False, []])
                e[0] = e[0] or urgent
                e[1].append(d)
        clock = 0
        for (kind, lo, width), (urgent, dsts) in sorted(groups.items(), key=lambda q: (not q[1][0], q[0][2], q[0])):
            free = None
            for d in dsts:
                e = set(engine_list(topo.mask(cores[s], cores[d])))
                free = e if free is None else free & e
            free = sorted(free)
            each = 1
            while each * 2 * len(dsts) <= len(free):
                each *= 2
            call = []
            for n, d in enumerate(dsts):
                call.append((kind, lo, lo + width, d, free[n::len(free) // each][:each]))
                clock += 512 + 2 * width
            for it in call:
                for q in ("ab" if kind == "m" else kind):
                    land[(q, s, it[3])] = ("r%s%d" % (kind, s), each)
                    eta[(q, s, it[3])] = clock
            calls[s].append(call)
    return own, parts, calls, land, eta


def rank_program(g, core, T, topo):
    r = T.rank_of(core)
    if r is None:
        return
    cores, sem, ab = T.cores, T.sem, T.ab
    own, parts, calls, land, eta = make_plan(cores, topo)
    mine = r * SLOT

    def when(x, d, k):
        return max(eta.get(("a", a_home(d // GC, k), x), 0), eta.get(("b", b_home(k, d % GC), x), 0))

    def ready(x, d):
        return max(when(x, d, k) for k in parts[(x, d)])

    give = sorted((ready(x, d), d) for (x, d) in parts if x == r)
    give = [d for t, d in give]
    take = sorted((ready(x, d), x) for (x, d) in parts if d == r)
    take = [x for t, x in take]

    g.sync.dma_start(ab[:, mine:mine + WA], T.a[:, :]).then_inc(sem.lda, 16)
    g.scalar.dma_start(ab[:, mine + WA:mine + SLOT], T.b[:, :]).then_inc(sem.ldb, 16)

    sent, loaded = 0, set()
    for call in calls[r]:
        for q in ("ab" if call[0][0] == "m" else call[0][0]):
            if q not in loaded:
                loaded.add(q)
                g.wait_ge(sem["ld" + q], 16)
        if len(call) == 1:
            kind, lo, hi, d, eng = call[0]
            rid, pid = topo.addr(cores[d], core)
            g.remote_dma(ab[:, mine + lo:mine + hi], ab[:, mine + lo:mine + hi], sem["r%s%d" % (kind, r)], sem.sent,
                         pid, rid, to_mask(eng))
            sent += len(eng)
        else:
            trs = []
            for kind, lo, hi, d, eng in call:
                rid, pid = topo.addr(cores[d], core)
                trs.append(RemoteDMATransfer(dst_ids=[DstId(rid=rid, pnc=pid)], dma_engine_mask=to_mask(eng),
                                             remote_sem=sem["r%s%d" % (kind, r)],
                                             src=ab[:, mine + lo:mine + hi], dst=ab[:, mine + lo:mine + hi]))
                sent += len(eng)
            g.remote_dma_fused(trs, local_sem=sem.sent)
    for n, d in enumerate(give):
        eng = engine_list(topo.mask(core, cores[d]))
        rid, pid = topo.addr(cores[d], core)
        g.wait_ge(sem["cpp%d" % n], 1)
        g.remote_dma(T.pin[:, r * F:(r + 1) * F], T.pout[:, n * F:(n + 1) * F], sem["rp%d" % r], sem.sent,
                     pid, rid, to_mask(eng))
        sent += len(eng)
    g.wait_ge(sem.sent, sent)

    jobs = []
    for n, d in enumerate(give):
        jobs += [(0, when(r, d, k), n, d, k) for k in parts[(r, d)]]
    jobs += [(1, when(r, r, k), NP, r, k) for k in own[r]]
    jobs.sort()
    left = {}
    for job in jobs:
        left[job[2]] = left.get(job[2], 0) + 1
    total = dict(left)
    waited = set()
    for late, t, n, d, k in jobs:
        i, j = d // GC, d % GC
        for kind, s in (("a", a_home(i, k)), ("b", b_home(k, j))):
            name, cnt = ("ld" + kind, 16) if s == r else land[(kind, s, r)]
            if name not in waited:
                waited.add(name)
                g.tensor.wait_ge(sem[name], cnt)
        ca = a_home(i, k) * SLOT + P * (k % KA)
        cb = b_home(k, j) * SLOT + WA + F * (k % KB)
        acc = T.accy if n == NP else T["accp%d" % n]
        first = left[n] == total[n]
        left[n] -= 1
        mm = g.tensor.matmul(acc[:, 0:F], ab[:, ca:ca + P], ab[:, cb:cb + F], first, left[n] == 0)
        if left[n] == 0:
            mm.then_inc(sem.mmy if n == NP else sem["mmp%d" % n], 1)

    for n, d in enumerate(give):
        g.vector.wait_ge(sem["mmp%d" % n], 1)
        g.vector.tensor_copy(T.pout[:, n * F:(n + 1) * F], T["accp%d" % n][:, 0:F]).then_inc(sem["cpp%d" % n], 1)
    g.vector.wait_ge(sem.mmy, 1)
    src = T.accy[:, 0:F]
    for n, x in enumerate(take):
        g.vector.wait_ge(sem["rp%d" % x], len(engine_list(topo.mask(cores[x], core))))
        if n + 1 < len(take):
            g.vector.tensor_tensor(T.tmp[:, :], src, T.pin[:, x * F:(x + 1) * F], AluOpType.add).then_inc(sem.yt, 1)
            g.vector.wait_ge(sem.yt, n + 1)
            src = T.tmp[:, :]
        else:
            g.vector.tensor_tensor(T.yo[:, :], src, T.pin[:, x * F:(x + 1) * F], AluOpType.add).then_inc(sem.yv, 1)
    if not take:
        g.vector.tensor_copy(T.yo[:, :], src).then_inc(sem.yv, 1)

    g.sync.wait_ge(sem.yv, 1)
    g.sync.dma_start(T.y[:, :], T.yo[:, :]).then_inc(sem.st, 16)
    g.sync.wait_ge(sem.st, 16)
